import numpy as np, ml_dtypes
CORES = [40,41,42,43,44,45,46,47]
N = 8
BF = ml_dtypes.bfloat16
W, C, DH, S = 2048, 256, 1024, 3
HI, LO, HA, HB = 9, 3, 1, 3
B, DB = W // C, DH // C
WT = np.array([37, 101, 59, 203, 83, 149, 11, 173, 67, 229, 127, 43, 191, 23, 251, 109])
def num(z):
    return np.sum(z * WT[:, None], axis=-2) & 4095
def place(u):
    return ((2741 * u) >> 5) & (DH - 1)
def pack(X, D, P, Q, z, l):
    a = np.ascontiguousarray
    return {"xr": a(X.reshape(N, 128, W)).astype(np.float32).astype(BF), "dr": a(D.reshape(N, 128, 2 * DH)).astype(np.int32),
            "pl": a(P.reshape(N, 128, C)).astype(np.int32), "ql": a(Q.reshape(N, 128, C)).astype(np.int32),
            "zq": a(z.reshape(N, 128, C)).astype(np.float32).astype(BF), "sd": a(l).astype(np.int32)}
def order(rng):
    return np.argsort(rng.random((8, W)), axis=1)
def over(pm):
    return np.broadcast_to(pm[None, :, None, :], (N, 8, 16, W))
def lay(pm, v):
    X = np.zeros((N, 8, 16, W), np.int64); np.put_along_axis(X, over(pm), v.astype(np.int64), 3)
    return X
def lanes(rng, pm, m):
    b = rng.integers(0, 16, (N, 8, 1, m)); t = rng.integers(0, W // 16, (N, 8, 16, m)); near = rng.random((N, 8, 1, m)) < 0.5
    return np.take_along_axis(over(pm), np.where(near, b * (W // 16) + t, rng.integers(0, W, (N, 8, 16, m))), 3)
def parts(rng):
    pm = order(rng)
    mid = np.repeat(rng.integers(60, 196, (N, 8, 16, 16)), W // 16, axis=3); amp = np.repeat(rng.choice(np.array([12.0, 40.0, 120.0]), (N, 8, 1, 16)), W // 16, axis=3)
    X = lay(pm, np.clip(np.floor(mid + amp * (2 * rng.random((N, 8, 16, W)) - 1)), 0, 255))
    return pm, X, lanes(rng, pm, 2 * DH), lanes(rng, pm, C), lanes(rng, pm, C), rng.integers(0, 256, (N, 8, 16, C)), rng.integers(0, 2, (N, 8, C))
def setup_inputs(rng):
    return pack(*parts(rng)[1:])
def setup_inputs_ends(rng):
    X = 255 * rng.integers(0, 2, (N, 8, 16, W)); dif = rng.choice(np.array([2, 3, 8, 16]), (N, 8)); dif[:, 7] = 16
    alt = np.argsort(rng.random((N, 8, 16)), axis=2) < dif[:, :, None]
    X[..., W - 1] = np.where(alt, 255 - X[..., 0], X[..., 0])
    cnt = rng.choice(np.array([0, LO - 1, LO, HI - 1, HI, 15, 16]), (N, 8, 1, 2 * DH))
    D = np.where(np.argsort(rng.random((N, 8, 16, 2 * DH)), axis=2) < cnt, W - 1, 0)
    kind = rng.integers(0, 3, (N, 8, 1, C)); Q = (W - 1) * np.where(kind == 2, rng.integers(0, 2, (N, 8, 16, C)), kind)
    P = (W - 1) * rng.integers(0, 2, (N, 8, 16, C)); l = rng.integers(0, 2, (N, 8, C))
    last = X[..., W - 1:]; half = np.argsort(rng.random((N, 8, 16, C)), axis=2) < 8; zk = rng.integers(0, 8, (N, 8, 1, C))
    z = 255 * rng.integers(0, 2, (N, 8, 16, C))
    z = np.where(zk == 0, 0, np.where(zk == 1, 255, np.where(zk == 2, 255 - last, np.where(zk == 3, X[..., :1], np.where(zk == 4, np.where(half, last, 255 - last), z)))))
    z[:, 7, :, C - 1] = 255 - X[:, 7, :, W - 1]; Q[:, 7, :, C - 1] = W - 1; l[:, 7, C - 1] = 1
    col = DH + place(num(z[:, 7, :, C - 1:]))[:, 0]
    for r in range(N): D[r, 7, :, col[r]] = W - 1
    return pack(X, D, P, Q, z, l)
def setup_inputs_corners(rng):
    pm = order(rng); V = W // 8; o = over(pm)
    b0 = rng.integers(2, 254, (N, 8, 16, 1)); b0[:, 1] = rng.integers(0, 3, (N, 16, 1)); b0[:, 6] = rng.integers(253, 256, (N, 16, 1))
    m = np.repeat(np.array([0, 0, 1, 2, 2, 3, 3, 4]), V)
    out = np.argsort(rng.random((N, 8, 16, W)), axis=2) < m
    by = 2 * rng.integers(0, 2, (N, 8, 16, W)) - 1; by = np.where(b0 == 0, 1, np.where(b0 == 255, -1, by))
    X = lay(pm, b0 + np.where(out, by, 0))
    cnt = rng.choice(np.array([0, LO - 1, LO, HI - 1, HI, 15, 16]), (N, 8, 1, 2 * DH)); odd = rng.random((N, 8, 1, 2 * DH)) < 0.35
    t = rng.integers(0, 2 * V, (N, 8, 16, 2 * DH)); t1 = t % V
    j = np.where(np.argsort(rng.random((N, 8, 16, 2 * DH)), axis=2) < cnt, np.where(odd, 2 * V + t1, 3 * V + t), np.where(odd, 3 * V + t1, 5 * V + t))
    D = np.take_along_axis(o, j, 3)
    own = B * np.arange(C) + rng.integers(0, B, (N, 8, 16, C)); ed = (W - 1) * rng.integers(0, 2, (N, 8, 16, C)); kind = rng.integers(0, 8, (N, 8, 1, C))
    Q = np.where(kind == 0, own, np.where(kind == 1, ed, np.take_along_axis(o, rng.integers(0, 2 * V, (N, 8, 16, C)), 3)))
    kind = rng.integers(0, 4, (N, 8, 1, C)); P = np.where(kind == 0, own, np.where(kind == 1, ed, np.take_along_axis(o, rng.integers(0, 8 * V, (N, 8, 16, C)), 3)))
    zk = rng.integers(0, 5, (N, 8, 1, C)); z = np.where(zk == 0, 0, np.where(zk == 1, 255, np.where(zk == 2, b0, rng.integers(0, 256, (N, 8, 16, C)))))
    l = (rng.random((N, 8, C)) < rng.choice(np.array([0.0, 0.5, 1.0]), (N, 8, 1))).astype(np.int64)
    return pack(X, D, P, Q, z, l)
def setup_inputs_crowd(rng):
    pm, X, D, P, Q, z, l = parts(rng)
    ix = np.zeros((8, C), np.int64)
    for g in (1, 3, 5, 7):
        e = C - 1 if g < 4 else int(rng.integers(1, C)); ix[g, e] = e
    w = np.broadcast_to(ix[None, :, None, :], (N, 8, 16, C))
    P, Q, z = [np.take_along_axis(v, w, 3) for v in (P, Q, z)]; l = np.take_along_axis(l, np.broadcast_to(ix[None], (N, 8, C)), 2)
    for v in (P, Q, z, l): v[1:, :2] = v[:1, :2]
    Q[:, 2:4] = Q[:, 2:4, :1].copy(); D[:, 2:4] = D[:, 2:4, :1].copy()
    D[:, 4:6] = Q[:, 4:6, :, :1]; D[:, 5, 15] = rng.integers(0, W, (N, 2 * DH))
    return pack(X, D, P, Q, z, l)
def setup_inputs_drops(rng):
    pm, X, D, P, Q, z, l = parts(rng); dg = (np.arange(8) % 3 != 2)[:, None, None]
    X1 = rng.integers(0, 101, X.shape); X1[..., W - 1] = 255
    Q1 = rng.integers(0, W - 1, Q.shape); z1 = rng.integers(0, 101, z.shape)
    if W == 4096:
        one = np.zeros((16, 1), np.int64); one[14] = 16; one[6] = 7
        pool = rng.integers(0, 101, (16, 32768)); pool = np.concatenate([one, pool[:, num(pool) >= 4064]], axis=1)
        high = np.argsort(rng.random((N, 8, 1, C)), axis=3) < C // 2
        z1 = np.where(high, np.moveaxis(pool[:, rng.integers(0, pool.shape[1], (N, 8, C))], 0, 2), z1)
        Q1 = np.where(high, rng.integers(W - 32, W - 1, Q.shape), Q1)
        z1[:, 7, :, C - 1] = one[:, 0]; Q1[:, 7, :, C - 1] = rng.integers(W - 32, W - 1, (N, 16)); Q1[:, 7, 15, C - 1] = 4075
    return pack(np.where(dg, X1, X), np.where(dg, W - 1, D), P, np.where(dg, Q1, Q), np.where(dg, z1, z), l)
def setup_inputs_spread(rng):
    e = rng.choice(np.array([1.0, 1.0, 3.0]), (N, 8, 1, 1))
    X = (np.exp2(8 * rng.random((N, 8, 1, W))) * rng.random((N, 8, 16, W))).astype(np.int64); z = (np.exp2(8 * rng.random((N, 8, 1, C))) * rng.random((N, 8, 16, C))).astype(np.int64)
    D, P, Q = [(W * rng.random((N, 8, 16, k)) ** e).astype(np.int64) for k in (2 * DH, C, C)]
    l = (rng.random((N, 8, C)) < rng.random((N, 8, 1))).astype(np.int64)
    return pack(X, D, P, Q, z, l)
def check_inputs(d):
    bad = []
    for k, lo, hi in (("xr", 0, 255), ("dr", 0, W - 1), ("pl", 0, W - 1), ("ql", 0, W - 1), ("zq", 0, 255), ("sd", 0, 1)):
        a = np.asarray(d[k]).astype(np.float64)
        if not (np.min(a) >= lo and np.max(a) <= hi): bad.append("range of " + k)
        elif np.any(a != np.floor(a)): bad.append("whole numbers in " + k)
    return bad
def go_on(v):
    h = C // 2
    return np.concatenate([np.roll(v[..., :h], HA, axis=0), np.roll(v[..., h:], HB, axis=0)], axis=-1)
def reference(xr, dr, pl, ql, zq, sd):
    X = xr.astype(np.float32).astype(np.int64).reshape(N, 8, 16, W); D = dr.astype(np.int64).reshape(N, 8, 16, 2 * DH)
    P = pl.astype(np.int64).reshape(N, 8, 16, C); Q = ql.astype(np.int64).reshape(N, 8, 16, C)
    z = zq.astype(np.float32).astype(np.int64).reshape(N, 8, 16, C); l = sd.astype(np.int64); A = np.zeros((N, 8, C), np.int64)
    c = np.arange(C); lane = np.arange(16)[:, None]
    for step in range(S):
        u = num(z)
        E = np.take_along_axis(D, (DH * l + place(u))[:, :, None, :], 3)
        x = np.take_along_axis(X, E.reshape(N, 8, 1, 16 * C), 3).reshape(N, 8, 16, 16, C)
        y = np.take_along_axis(X, Q.reshape(N, 8, 1, 16 * C), 3).reshape(N, 8, 16, 16, C)
        lo = np.min(y, axis=3); hi = np.max(y, axis=3)
        rows = np.sum((lo[:, :, :, None, :] <= x) & (x <= hi[:, :, :, None, :]), axis=2)
        ok = rows >= 14 + (A & 1)[:, :, None, :]; n = np.sum(ok, axis=2)
        dist = np.sum(np.abs(x - z[:, :, :, None, :]), axis=2)
        beta = np.argmin(np.where(ok, dist, 2 ** 20), axis=2)
        xb = np.take_along_axis(x, beta[:, :, None, None, :], 3)[:, :, :, 0, :]
        P1 = np.where(ok, E, P); made = (((Q * u[:, :, None, :]) >> 5) + Q + 37 * lane) & (W - 1)
        cont = (n >= HI)[:, :, None, :]; drop = (n < LO)[:, :, None, :]
        z = np.where(cont, np.abs(z - xb), np.where(drop, np.abs(z - hi), (z + xb) >> 1))
        u1 = num(z)
        dc = (DH * (1 - l) + DB * c + (u1 & (DB - 1)))[:, :, None, :]
        np.put_along_axis(D, dc, np.where(cont, P1, np.take_along_axis(D, dc, 3)), 3)
        xc = (B * c + (u1 & (B - 1)))[:, :, None, :]
        np.put_along_axis(X, xc, (np.take_along_axis(X, xc, 3) + z) >> 1, 3)
        P, Q = np.where(cont, P1, Q), np.where(cont, Q, np.where(drop, made, P1))
        l = np.where(n >= HI, l, 1 - l); A = A + (n < LO)
        if step < S - 1: P, Q, z, l, A = [go_on(v) for v in (P, Q, z, l, A)]
    return {"yx": X.reshape(N, 128, W).astype(np.float32).astype(BF), "yd": D.reshape(N, 128, 2 * DH).astype(np.float32), "yp": P.reshape(N, 128, C).astype(np.float32),
            "yq": Q.reshape(N, 128, C).astype(np.float32), "yz": z.reshape(N, 128, C).astype(np.float32).astype(BF), "ys": (2 * A + l).astype(np.float32)}

from concourse.bass import DstId, RemoteDMATransfer
from concourse.mybir import AluOpType as ALU, AxisListType as AX, ActivationFunctionType as AF

WT = [37, 101, 59, 203, 83, 149, 11, 173, 67, 229, 127, 43, 191, 23, 251, 109]
HOP = [1, 3]
STEPS = 3
CFG = {"y": [[[("S", 32), ("V", 32), ("S", 64)], [("S", 64), ("S", 64)]]] + [[[("S", 32), ("S", 32), ("S", 64)], [("S", 64), ("S", 64)]]] * 2,
       "x": [[[("V", 80), ("S", 48)], [("S", 64), ("S", 64)]]] * 3,
       "oldS": [0, 0], "aS": [1, 1], "nS": [[0, 0], [0, 0], [0, 0]],
       "dPE": [[0, 0]] * 3, "p1S": [0, 0], "gconv": 1, "merge": [0, 0], "vS": [0, 1]}
BFP = ""
MID = {"gf": 1.56, "sf": 3.8, "pe": 0.45, "fx": 20.0, "bw": 200.0, "rl": 2500.0, "sem": 80.0}
BIAS = {x.split(":")[0]: 100 * int(x.split(":")[1]) for x in """
e00V:-55 e01V:68 e10V:-125 e11V:218 e20V:42 e21V:51 initS:-104 initT:219 initV:2 m00S:213 m00T:222 m00V:221 m01S:116 m01T:21 m10S:445 m10T:295 m10V:255 m11S:153 m11V:-31 m20S:269 m20T:126 m20V:220 m21S:144 m21T:-48 m21V:-4 p00S:205 p00T:-219 p00V:-47 p01S:202 p01T:-143 p01V:-27 p10S:497 p10T:-125 p10V:-5 p11S:-18 p11T:-110 p11V:-16 p20S:242 p20T:-198 p20V:-65 p21S:-11 p21T:-7 p21V:-272 sc00V:388 sc01V:-72 sc10V:348 sc11V:-46 sc20V:395 sc21V:-185 t00S:-118 t00T:116 t00V:1 t01S:402 t01T:-91 t01V:41 t10S:6 t10T:4 t10V:1 t11S:505 t11T:-167 t11V:161 t20S:121 t20T:-32 t20V:4 t21S:562 t21T:-122 t21V:177 w00V:1 w01S:-82 w01V:339 w10V:-13 w11S:-82 w11V:367 w20V:89 w21S:22 w21V:219 x00S:7 x00V:443 x01S:-590 x10S:25 x10V:44 x11S:-345 x20S:-13 x20V:23 x21S:-472 y00S:229 y00V:150 y01S:-112 y10S:-32 y10V:70 y11S:-177 y20S:16 y20V:37 y21S:-195
""".split()}
LOOK = (250.0, 0.5)
F, B, I, U = "float32", "bfloat16", "int32", "uint16"

SCRATCH = {}


def _sb(name, n, dtype):
    SCRATCH[name] = ("sbuf", [128, n], dtype)


for _n, _w, _d in [("X", 2048, B), ("Di", 2048, I), ("Df", 3072, F), ("Dst", 2560, F), ("Qi", 256, I), ("Pi", 256, I),
                   ("sdi", 256, I), ("sdb", 256, B), ("colf", 160, F), ("blk", 128, F), ("pint", 8, I), ("pc", 16, F),
                   ("wrow", 48, F), ("Ipad", 160, B), ("Ia0", 160, B), ("Ia1", 160, B), ("Bf", 144, B), ("Bh", 144, B), ("Bw", 144, B),
                   ("Sel", 144, B), ("Wb", 128, B), ("SI", 1152, B), ("I32", 256, F), ("mk1", 1024, B), ("mk2", 1024, B), ("mkk", 128, F),
                   ("kc", 128, B), ("dg", 128, B), ("dgf", 128, F), ("cw", 8, F), ("cb", 80, B), ("c8", 8, I), ("cc", 384, B), ("tab", 16, B), ("yso", 256, F)]:
    _sb(_n, _w, _d)
for _h in range(2):
    for _n, _w, _d in [("y", 2048, B), ("x", 2048, B), ("hiS", 2048, B), ("loS", 2048, B), ("ge", 2048, B), ("le", 2048, B),
                       ("ab", 2048, B), ("Eu", 128, U), ("diff", 128, F), ("tf", 512, F), ("ti", 512, I), ("tb", 512, B),
                       ("zm", 128, F), ("zw", 384, B), ("kT", 256, F), ("wi", 72, I), ("wb", 48, B), ("ou", 32, U)]:
        _sb(_n + str(_h), _w, _d)
    for _s in range(STEPS):
        for _n, _w, _d in [("RU", 176, U), ("RB", 176, B), ("RF", 512, F), ("SU", 176, U), ("SB", 176, B), ("SF", 256, F)]:
            _sb("%s%d%d" % (_n, _s, _h), _w, _d)
for _n in ["Plo", "Phi", "Pd0", "Pd1", "Pcn", "Pdk", "Pw", "Pu"]:
    SCRATCH[_n] = ("psum", [128, 1024], B) if BFP and _n in ("Plo", "Phi") else ("psum", [128, 512], F)
DRAM = {"xr": B, "dr": I, "pl": I, "ql": I, "zq": B, "sd": I, "yx": B, "yd": F, "yp": F, "yq": F, "yz": B, "ys": F}
SIZE = {F: 4, B: 2, I: 4, U: 2}


def A(name, a, b, step=1, p0=0, p1=128):
    return ("ap", name, a, b, step, p0, p1)


def IND(win, off):
    return ("ind", win, off)


def _isap(v):
    return isinstance(v, tuple) and len(v) > 0 and v[0] in ("ap", "ind")


def _dt(ap):
    n = ap[1][1] if ap[0] == "ind" else ap[1]
    return DRAM[n] if n in DRAM else SCRATCH[n][2]


def _ps(ap):
    return ap[0] == "ap" and ap[1] in SCRATCH and SCRATCH[ap[1]][0] == "psum"


def _n(ap):
    if ap[0] == "ind":
        return 16 * (ap[2][3] - ap[2][2])
    return len(range(ap[2], ap[3], ap[4]))


def _regs(ap):
    if ap[0] == "ind":
        return [ap[1][1:4]], [ap[2][1:4]]
    return [ap[1:4]], []


def costs(ops, sc):
    gf, sf, pe, fx, bw = sc["gf"], sc["sf"], sc["pe"], sc["fx"], sc["bw"]
    out = []
    for o in ops:
        k, n = o["feat"]
        if k == "d":
            out.append((100.0, n / bw))
        elif k == "r":
            out.append((500.0, sc["rl"]))
        elif k == "n":
            out.append((0.0, 0.0))
        else:
            c = {"pe": n * pe, "cy": fx + n * 0.83, "ga": 55 + gf * n * 0.83, "sc": 50 + sf * n * 0.83}[k]
            out.append((1.25 * c, 0.0))
    return out


def place(ops, j, cl, sc, free, done, pipe):
    o = ops[j]
    st = max([free[o["eng"]]] + [done[i] + (sc["sem"] if w else 0.0) for i, w in o["deps"].items()])
    free[o["eng"]] = st + cl[j][0]
    if o["kind"] == "d":
        pipe[0] = max(pipe[0], st + cl[j][0] + 2000) + cl[j][1]
        done[j] = pipe[0]
    else:
        done[j] = st + cl[j][0] + cl[j][1]
    return st


def span(ops, order, sc):
    cl, free, done, pipe = costs(ops, sc), {e: 0.0 for e in "VSTGYN"}, [0.0] * len(ops), [0.0]
    for j in order:
        place(ops, j, cl, sc, free, done, pipe)
    return max(done)


def schedule(ops, sc, bias, look):
    n, cl, SEM = len(ops), costs(ops, sc), sc["sem"]
    succ = [[] for _ in range(n)]
    for j, o in enumerate(ops):
        for i in o["deps"]:
            succ[i].append(j)
    prio = [0.0] * n
    for j in range(n - 1, -1, -1):
        prio[j] = cl[j][0] + cl[j][1] + (2000 if ops[j]["kind"] == "d" else 0) + max([prio[k] + (SEM if ops[k]["deps"][j] else 0.0) for k in succ[j]] + [0.0])
    prio = [prio[j] + bias.get(ops[j]["tag"], 0.0) + ops[j].get("first", 0.0) for j in range(n)]
    free = {e: 0.0 for e in "VSTGYN"}
    done, left = [0.0] * n, [len(o["deps"]) for o in ops]
    rdy = {j: 0.0 for j in range(n) if left[j] == 0}
    order, pipe = [], [0.0]
    while rdy:
        st = {j: max(t, free[ops[j]["eng"]]) for j, t in rdy.items()}
        j0 = min(st, key=lambda j: (st[j], -prio[j], j))
        e = ops[j0]["eng"]
        lim = st[j0] + min(look[0], look[1] * cl[j0][0])
        j = min((k for k in st if ops[k]["eng"] == e and st[k] <= lim), key=lambda k: (-prio[k], k))
        ops[j]["t0"] = place(ops, j, cl, sc, free, done, pipe)
        ops[j]["cost"] = cl[j][0]
        order.append(j)
        del rdy[j]
        for k in succ[j]:
            left[k] -= 1
            if left[k] == 0:
                rdy[k] = max(done[i] + (SEM if w else 0.0) for i, w in ops[k]["deps"].items())
    return order


def build(CFG):
    ops = []
    tag = ["init"]

    def add(eng, meth, out, args, kw=None, kind="c", extra=None):
        kw = kw or {}
        wr, rd = _regs(out) if out is not None else ([], [])
        wr, rd = list(wr), list(rd)
        aps = [a for a in list(args) + list(kw.values()) if _isap(a)]
        for a in aps:
            m, o = _regs(a)
            rd += m + o
        allap = aps + ([out] if out is not None else [])
        if kind == "c":
            n = _n(out)
            two = all(SIZE[_dt(a)] == 2 for a in allap if _n(a) > 1)
            if eng == "T":
                feat = ("pe", max(min(64, _n(args[0])), _n(args[1])) * (4 if _dt(args[0]) == F else 1))
            elif eng == "G":
                feat = ("cy", 200 + 2 * n)
            elif out[0] == "ind":
                feat = ("sc", n)
            elif any(a[0] == "ind" for a in aps):
                feat = ("ga", n)
            elif meth == "tensor_tensor":
                feat = ("cy", max(64, n * (1 if any(_ps(a) for a in aps[:2]) else 2)))
            elif meth in ("activation", "tensor_reduce"):
                feat = ("cy", max(64, _n(aps[0])))
            else:
                feat = ("cy", max(64, n * (0.5 if two else 1)))
        elif kind == "d":
            feat = ("d", _n(out) * SIZE[_dt(out)] * (out[6] - out[5]))
        else:
            feat = (kind, 0)
        banks = sorted(set(a[1] for a in allap if _ps(a)))
        ops.append(dict(eng=eng, meth=meth, out=out, args=list(args), kw=kw, kind=kind, rd=rd, wr=wr, feat=feat,
                        banks=banks, extra=extra, after=[], tag=tag[0] + eng))
        return len(ops) - 1

    def cp(o, i): return add("V", "tensor_copy", o, [i])
    def tt(o, a, b, op): return add("V", "tensor_tensor", o, [a, b, op])
    def ts(o, a, s1, op0, s2=None, op1=None):
        return add("V", "tensor_scalar", o, [a, s1, s2, op0] + ([op1] if op1 is not None else []))
    def ms(o, v): return add("V", "memset", o, [v])
    def act(o, i, f, bias=None, scale=None):
        kw = {}
        if bias is not None: kw["bias"] = bias
        if scale is not None: kw["scale"] = scale
        return add("S", "activation", o, [i, f], kw)
    def mmg(o, pairs):
        for j, (l, r) in enumerate(pairs):
            add("T", "matmul", o, [l, r, j == 0, j == len(pairs) - 1])
    def conv(o, i):
        if CFG["gconv"]:
            return add("G", "affine_select", o, [i, [[0, _n(o)]], ALU.is_ge, 0.0, 0, 0])
        return cp(o, i)
    def dma(q, o, i): return add(q, "dma_start", o, [i], kind="d")
    def iota(o, pat, base, cm, fl=True):
        return add("G", "iota", o, [pat, base, cm], {"allow_small_or_imprecise_dtypes": True} if fl else {})

    l1 = [dma("Y", A("Qi", 0, 256), A("ql", 0, 256)), dma("Y", A("X", 0, 2048), A("xr", 0, 2048)),
          dma("Y", A("Di", 0, 2048), A("dr", 0, 2048)), dma("Y", A("Pi", 0, 256), A("pl", 0, 256))]
    l2 = [dma("S", A("sdi", 0, 256, 1, 0, 8), A("sd", 0, 256, 1, 0, 8))]
    l2 += [dma("S", A("RB0%d" % h, 0, 128), A("zq", 128 * h, 128 * h + 128)) for h in range(2)]
    for lst in (l1, l2):
        for k, a in enumerate(lst):
            ops[a]["first"] = 1.0e7 - 1.0e6 * k + (5.0e5 if lst is l2 else 0.0)
    iota(A("pint", 0, 1), [[1, 1]], 0, 1, False)
    iota(A("colf", 0, 160), [[1, 160]], 0, 0)
    iota(A("pc", 5, 6), [[1, 1]], 16, 1)
    iota(A("pc", 7, 8), [[1, 1]], 15, 16)
    iota(A("blk", 0, 128), [[1, 8], [0, 16]], 0, 0)
    for i, w in enumerate(WT):
        ms(A("wrow", i, i + 1), float(w))
    ts(A("pint", 1, 2), A("pint", 0, 1), 15, ALU.bitwise_and)
    ts(A("pint", 2, 3), A("pint", 0, 1), 4, ALU.arith_shift_right)
    ts(A("pint", 3, 4), A("pint", 0, 1), 4, ALU.arith_shift_right, 1, ALU.bitwise_and)
    cp(A("pc", 0, 4), A("pint", 0, 4))
    pc = lambda j: A("pc", j, j + 1)
    ts(A("wrow", 16, 32), A("colf", 0, 16), pc(1), ALU.is_equal)
    tt(A("wrow", 32, 48), A("wrow", 16, 32), A("wrow", 0, 16), ALU.mult)
    add("V", "tensor_reduce", pc(10), [A("wrow", 32, 48), AX.X, ALU.add])
    ts(pc(4), pc(2), 16.0, ALU.mult, 15.0, ALU.add)
    ts(pc(6), pc(3), -16.0, ALU.mult, 16.0, ALU.add)
    ts(pc(11), pc(3), 16.0, ALU.mult)
    ts(pc(8), pc(1), 0.0625, ALU.mult, -0.46875, ALU.add)
    ts(pc(9), pc(1), 1184.0, ALU.mult)
    ts(A("Bw", 0, 144), A("colf", 0, 144), pc(4), ALU.is_equal, pc(10), ALU.mult)
    ts(A("Bf", 0, 144), A("colf", 0, 144), pc(4), ALU.is_equal)
    ts(A("Sel", 0, 144), A("colf", 0, 144), pc(7), ALU.is_equal)
    ops[ts(A("Ipad", 0, 160), A("colf", 0, 160), pc(5), ALU.is_equal)]["first"] = 1.0e5
    ts(A("Ia0", 0, 160), A("colf", 0, 160), pc(5), ALU.is_equal, pc(6), ALU.mult)
    ts(A("Ia1", 0, 160), A("colf", 0, 160), pc(5), ALU.is_equal, pc(11), ALU.mult)
    ts(A("Wb", 0, 128), A("blk", 0, 128), pc(2), ALU.is_equal, pc(10), ALU.mult)
    used = sorted(set(v for row in CFG["nS"] for v in row))
    if used[-1] > 0:
        act(A("Bh", 0, 144), A("Bf", 0, 144), AF.Copy, scale=0.5)
    if any(0 < v < 4 for v in used):
        ts(A("pint", 4, 5), A("pint", 0, 1), 3, ALU.bitwise_and)
    for v in used:
        if 0 < v < 4:
            ts(pc(15), A("pint", 4, 5), float(v), ALU.is_lt, 8.0, ALU.mult)
            ts(pc(11 + v), pc(15), -29.5, ALU.add)
    ID = A("Ipad", 16, 144)
    SC = {}
    for j, v in enumerate([-1, -4096, -8192, 64, -64, -768, -256, 512, -0.5]):
        SC[v] = A("SI", 128 * j, 128 * j + 128)
        act(SC[v], ID, AF.Copy, scale=float(v))
    if any(any(r) for r in CFG["dPE"]):
        act(A("I32", 0, 128), ID, AF.Copy)
        act(A("I32", 128, 256), ID, AF.Copy, scale=-1.0)
    ms(A("mk1", 0, 1024), 0.0)
    ms(A("mk1", 0, 1024, 16), 256.0)
    act(A("mk2", 0, 1024), A("mk1", 0, 1024), AF.Identity, bias=256.0, scale=-1.0)
    ms(A("mkk", 0, 128), -1.0e6)
    ms(A("mkk", 0, 128, 16), 1.0e6)
    ts(A("kc", 0, 128), A("colf", 0, 128), 0.0, ALU.mult, pc(8), ALU.add)
    if any(CFG["vS"]):
        iota(A("dgf", 0, 128), [[0, 8], [1, 16]], 0, 0)
        ts(A("dg", 0, 128), A("dgf", 0, 128), pc(1), ALU.not_equal, 524288.0, ALU.mult)
    cw = A("cw", 0, 8)
    ops[ts(cw, A("colf", 0, 8), 16.0, ALU.mult, pc(1), ALU.add)]["first"] = 1.0e5
    cb = lambda j: A("cb", 8 * j, 8 * j + 8)
    for j, (m, a) in enumerate([(1, 64), (1, 128), (16, 0), (4, 0), (4, 512), (0, 1280), (0, 512), (0, 0.5), (8, 0)]):
        act(cb(j), cw, AF.Identity, bias=float(a), scale=float(m))
    ts(A("c8", 0, 8), cw, 8.0, ALU.mult)
    ms(A("cc", 0, 128), 557056.0)
    ms(A("cc", 128, 256), 32.0)
    ms(A("cc", 256, 384), -0.5)
    ms(A("tab", 0, 16), 0.0)
    ms(A("tab", 1, 2), -1.0)
    R = lambda k: A("Bf", 15 - k, 143 - k)
    RW = lambda k: A("Bw", 15 - k, 143 - k)

    def column(h, vi, dst_p):
        u, t = A("wi%d" % h, 8, 16), A("wi%d" % h, 16, 24)
        ts(u, vi, 4095, ALU.bitwise_and)
        ts(t, u, 2741.0, ALU.mult)
        ts(dst_p, t, 5, ALU.arith_shift_right, 1023, ALU.bitwise_and)

    ts(A("sdb", 0, 256, 1, 0, 8), A("sdi", 0, 256, 1, 0, 8), 1024.0, ALU.mult)
    for h in range(2):
        cp(A("RU0%d" % h, 0, 128), A("Qi", 128 * h, 128 * h + 128))
    mmg(A("Pw", 16, 32), [(A("Sel", 15 - r, 143 - r, 1, 0, 8), A("sdb", r, 256, 16, 0, 8)) for r in range(16)])
    for h in range(2):
        mmg(A("Pw", 8 * h, 8 * h + 8), [(RW(r), A("RB0%d" % h, r, 128, 16)) for r in range(16)])
    for h in range(2):
        vi = A("wi%d" % h, 0, 8)
        cp(vi, A("Pw", 8 * h, 8 * h + 8))
        column(h, vi, A("wi%d" % h, 24, 32))
        tt(A("wi%d" % h, 32, 40), A("wi%d" % h, 24, 32), A("Pw", 16 + 8 * h, 24 + 8 * h), ALU.add)
        cp(A("RU0%d" % h, 168, 176), A("wi%d" % h, 32, 40))
    for h in range(2):
        act(A("RB0%d" % h, 128, 136), A("Pw", 16 + 8 * h, 24 + 8 * h), AF.Identity, bias=-1.0, scale=1.0 / 512)
        ms(A("RB0%d" % h, 136, 144), 1.0)
        ms(A("RB0%d" % h, 144, 152), 0.0)
        conv(A("RF0%d" % h, 128, 256), A("Qi", 128 * h, 128 * h + 128))
        if CFG["dPE"][0][h]:
            conv(A("RF0%d" % h, 0, 128), A("Pi", 128 * h, 128 * h + 128))
        for s in range(STEPS - 1):
            act(A("SB%d%d" % (s, h), 152, 176), A("colf", 0, 24), AF.Copy)
    tag[0] = "cv"
    for j in range(4):
        conv(A("Df", 512 * j, 512 * j + 512), A("Di", 512 * j, 512 * j + 512))

    X = A("X", 0, 2048)
    for s in range(STEPS):
        last = s == STEPS - 1
        nm = lambda n, h: "%s%d%d" % (n, s, h)
        if last:
            for a in (0, 1024):
                dma("Y", A("Dst", a, a + 512), A("Df", a, a + 512))
        Dw = A("Di" if s == 0 else "Df", 0, 2048)
        Pof = lambda h: A("Pi", 128 * h, 128 * h + 128) if s == 0 else A(nm("RF", h), 0, 128)

        def pre(h):
            H = str(h)
            RU, RB, RF = nm("RU", h), nm("RB", h), nm("RF", h)
            z = A(RB, 0, 128)
            tag[0] = "e%d%d" % (s, h)
            col = A(RU, 168, 176)
            cp(A("Eu" + H, 0, 128), IND(Dw, col))
            tag[0] = "p%d%d" % (s, h)
            if CFG["dPE"][s][h]:
                act(A("diff" + H, 0, 128), IND(A("Df", 0, 2048), col), AF.Copy)
            else:
                tt(A("diff" + H, 0, 128), IND(Dw, col), Pof(h), ALU.subtract)
            mmg(A("Pu", 0, 128), [(A("Wb", 0, 128), z)])
            act(A("tb" + H, 0, 128), A("Pu", 0, 128), AF.Identity, bias=135.5 + 1.0 / 8192, scale=1.0 / 4096)
            mmg(A("Pu", 128, 256), [(A("Wb", 0, 128), z), (ID, A("cc", 0, 128)), (ID, A("cc", 128, 256)), (SC[-4096], A("tb" + H, 0, 128))])
            tt(A("tf" + H, 0, 128), A(RF, 128, 256), A("Pu", 128, 256), ALU.mult)
            ts(A("ti" + H, 0, 128), A("tf" + H, 0, 128), pc(9), ALU.add)
            ts(A("ti" + H, 128, 256), A("ti" + H, 0, 128), 5, ALU.arith_shift_right, 2047, ALU.bitwise_and)
            conv(A(RF, 384, 512), A("ti" + H, 128, 256))
            if not CFG["aS"][h]:
                act(A("zm" + H, 0, 128), z, AF.Identity, bias=-0.5)
            if s > 0:
                act(A("tb" + H, 128, 256), IND(A("tab", 0, 16), A(RU, 144, 152)), AF.Copy)

        def gathers(h):
            H = str(h)
            RU = nm("RU", h)
            for dst, lst in (("y", RU), ("x", "Eu" + H)):
                q = 0
                for e, nq in CFG[dst][s][h]:
                    tag[0] = "%s%d%d" % (dst, s, h)
                    a, b = 16 * q, 16 * (q + nq)
                    if e == "S":
                        act(A(dst + H, a, b), IND(X, A(lst, q, q + nq)), AF.Copy)
                    else:
                        cp(A(dst + H, a, b), IND(X, A(lst, q, q + nq)))
                    if dst == "y":
                        tag[0] = "sc%d%d" % (s, h)
                        add("V", "tensor_tensor_scan", A("hiS" + H, a, b), [A("mk2", 0, b - a), A("y" + H, a, b), 0.0, ALU.min, ALU.max])
                        add("V", "tensor_tensor_scan", A("loS" + H, a, b), [A("mk1", 0, b - a), A("y" + H, a, b), 0.0, ALU.max, ALU.min])
                    q += nq

        def main(h):
            H = str(h)
            tag[0] = "m%d%d" % (s, h)
            z = A(nm("RB", h), 0, 128)
            lo, hi = A("loS" + H, 15, 2048, 16), A("hiS" + H, 15, 2048, 16)
            ns = CFG["nS"][s][h]
            for P_, src in (("Phi", hi), ("Plo", lo)):
                for i in range(4 if ns < 4 or P_ == "Phi" else 0):
                    if not BFP:
                        mmg(A(P_, i, 512, 4), [(ID, src)])
                    elif BFP[i] == "S":
                        act(A(P_, i, 512, 4), src, AF.Copy)
                    else:
                        cp(A(P_, i, 512, 4), src)
            mmg(A("Pu", 256, 384), [(ID, hi), (SC[-1], z)])
            act(A("zw" + H, 256, 384), A("Pu", 256, 384), AF.Abs, scale=2.0)
            for b in range(4):
                bank = "Pd%d" % (b % 2)
                for i in range(4):
                    mmg(A(bank, 128 * i, 128 * i + 128), [(ID, A("x" + H, 4 * b + i, 2048, 16)), (SC[-1], z)])
                act(A("ab" + H, 512 * b, 512 * b + 512), A(bank, 0, 512), AF.Abs)
            pairs = [(ID, A("tb" + H, 128, 256))] if s > 0 else []
            late = []
            for j in range(4):
                for nme, P_, op in (("ge", "Plo", ALU.is_ge), ("le", "Phi", ALU.is_le)):
                    if nme == "ge" and j < ns:
                        bank = "Pd%d" % (j % 2)
                        tag[0] = "g%d%d" % (s, h)
                        for i in range(4):
                            mmg(A(bank, 128 * i, 128 * i + 128), [(ID, A("x" + H, j + 4 * i, 2048, 16)), (SC[-1], lo)])
                        act(A(nme + H, 512 * j, 512 * j + 512), A(bank, 0, 512), AF.Sign, bias=0.5)
                        tag[0] = "m%d%d" % (s, h)
                        late += [(A("Bh", 15 - j - 4 * i, 143 - j - 4 * i), A(nme + H, 512 * j + 128 * i, 512 * j + 128 * i + 128)) for i in range(4)]
                        continue
                    tt(A(nme + H, 512 * j, 512 * j + 512), A("x" + H, j, 2048, 4), A(P_, 0, 512), op)
                    pairs += [(R(j + 4 * i), A(nme + H, 512 * j + i, 512 * j + 512, 4)) for i in range(4)]
            cut = len(pairs) - 4
            mmg(A("Pcn", 0, 128), pairs[:cut] + late + pairs[cut:])
            sg = A("tb" + H, 256, 384)
            act(sg, A("Pcn", 0, 128), AF.Sign, bias=-29.5 if ns == 0 else -21.5 if ns == 4 else pc(11 + ns))
            mmg(A("Pdk", 0, 128), [(ID, A("kc", 0, 128))] + [(R(k), A("ab" + H, 128 * k, 128 * k + 128)) for k in range(16)] + [(SC[-8192], sg)])

        def tail(h):
            H = str(h)
            RU, RB, RF, SU, SB, SF = [nm(n, h) for n in ("RU", "RB", "RF", "SU", "SB", "SF")]
            z, sg = A(RB, 0, 128), A("tb" + H, 256, 384)
            wi = lambda a, n=8: A("wi" + H, a, a + n)
            wb = lambda a, n=8, st=1: A("wb" + H, a, a + n, st)
            ou = lambda a, n=8: A("ou" + H, a, a + n)
            tag[0] = "t%d%d" % (s, h)
            mmg(A("Pw", 0, 8), [(R(r), A("tb" + H, 256 + r, 384, 16)) for r in range(16)])
            sc, sd = wb(0), wb(8)
            act(sc, A("Pw", 0, 8), AF.Sign, bias=-1.0)
            act(sd, A("Pw", 0, 8), AF.Sign, bias=11.0)
            mmg(A("Pw", 16, 24), [(ID, cb(0)), (SC[64], sc)])
            mmg(A("Pw", 24, 32), [(ID, cb(1)), (SC[-64], sc), (SC[-64], sd)])
            tt(A(SB, 128, 144), A(RB, 128, 144), wb(0, 16), ALU.mult)
            if not last:
                mmg(A("Pw", 32, 40), [(ID, cb(7)), (SC[-0.5], A(SB, 136, 144))])
            cp(A(SU, 128, 144 if last else 152), A("Pw", 16, 32 if last else 40))
            mmg(A("Pw", 8, 16), [(ID, A(RB, 144, 152)), (ID, sd)])
            merge = CFG["merge"][h]
            if merge:
                mmg(A("Pw", 40, 48), [(ID, cb(8))])
            mmg(A("Pw", 48, 56), [(ID, cb(3 + h)), (ID, cb(5)), (SC[-768], sc), (SC[-256], A(RB, 128, 136)), (SC[-256], A(SB, 128, 136))])
            if not last:
                mmg(A("Pw", 56, 64), [(ID, cb(6)), (SC[512], A(SB, 128, 136))])
            act(A(SB, 144, 152), A("Pw", 8, 16), AF.Copy)
            add("V", "transpose", A("kT" + H, 0, 128), [A("Pdk", 0, 128)])
            add("V", "tensor_tensor_scan", A("kT" + H, 128, 256), [A("mkk", 0, 128), A("kT" + H, 0, 128), 0.0, ALU.max, ALU.min])
            ks = A("kT" + H, 143, 256, 16)
            ts(A("kT" + H, 0, 8), ks, 12582912.0, ALU.add, 12582912.0, ALU.subtract)
            tt(wb(16), ks, A("kT" + H, 0, 8), ALU.subtract)
            b0, b1 = A("wb" + H, 16, 24, 2), A("wb" + H, 17, 24, 2)
            mmg(A("Pu", 384, 392, 2), [(ID, A("cb", 16, 24, 2)), (A("Ia0", 16, 144), b0), (A("Ia0", 0, 128), b1)])
            mmg(A("Pu", 385, 392, 2), [(ID, A("cb", 17, 24, 2)), (A("Ia1", 32, 160), b0), (A("Ia1", 16, 144), b1)])
            ts(ou(0), A("Pu", 384, 392), 7.5, ALU.add)
            pok, pm, pd, psum = ([A("Pcn", 128, 256), A("Pcn", 256, 384), A("Pcn", 384, 512), A("Pdk", 128, 256)] if h else
                                 [A("Pw", 320, 448), A("Pw", 192, 320), A("Pw", 320, 448), A("Pu", 0, 128)])
            if CFG["dPE"][s][h]:
                ok, Pf = A("tb" + H, 0, 128), A(RF, 0, 128)
                act(ok, sg, AF.Relu)
                mmg(pm, [(A("I32", 0, 128), A("diff" + H, 0, 128)), (A("I32", 128, 256), Pf)])
                if CFG["p1S"][h]:
                    tt(A("tf" + H, 384, 512), pm, ok, ALU.mult)
                    mmg(pok, [(A("I32", 0, 128), Pf), (A("I32", 0, 128), A("tf" + H, 384, 512))])
                    act(A(RF, 256, 384), pok, AF.Copy)
                else:
                    tt(pok, pm, ok, ALU.mult)
                    tt(A(RF, 256, 384), pok, Pf, ALU.add)
            else:
                act(pok, sg, AF.Relu)
                tt(pm, A("diff" + H, 0, 128), pok, ALU.mult)
                tt(A(RF, 256, 384), pm, Pof(h), ALU.add)
            act(A(SF, 0, 256), IND(A(RF, 128, 512), A(SU, 128, 144)), AF.Copy)
            if not last:
                cp(A(SU, 0, 128), A(SF, 128, 256))
            xw, ta = IND(A("x" + H, 0, 2048), ou(0)), A("tb" + H, 384, 512)
            if CFG["aS"][h]:
                act(ta, xw, AF.Copy)
                mmg(psum, [(ID, A("cc", 256, 384)), (ID, z), (ID, ta)])
                mmg(pd, [(SC[-1], z), (ID, ta)])
                ts(A("zw" + H, 128, 256), psum, 25165824.0, ALU.add, 25165824.0, ALU.subtract)
                act(A("zw" + H, 0, 128), pd, AF.Abs, scale=2.0)
            else:
                tt(ta, xw, z, ALU.subtract)
                act(A("zw" + H, 0, 128), ta, AF.Abs, scale=2.0)
                tt(A("tf" + H, 128, 256), xw, A("zm" + H, 0, 128), ALU.add)
                ts(A("zw" + H, 128, 256), A("tf" + H, 128, 256), 25165824.0, ALU.add, 25165824.0, ALU.subtract)
            zn = A(SB, 0, 128)
            act(zn, IND(A("zw" + H, 0, 384), A(SU, 136, 144)), AF.Copy, scale=0.5)
            vi = wi(0)
            if CFG["vS"][h]:
                mmg(A("Pu", 128, 256), [(ID, A("dg", 0, 128)), (A("Wb", 0, 128), zn)])
                add("V", "tensor_tensor_scan", A("kT" + H, 128, 256), [A("mkk", 0, 128), A("Pu", 128, 256), 0.0, ALU.max, ALU.min])
                cp(vi, ks)
            else:
                mmg(A("Pu", 392, 400), [(RW(r), A(SB, r, 128, 16)) for r in range(16)])
                cp(vi, A("Pu", 392, 400))
            ts(wi(24), vi, 7, ALU.bitwise_and)
            if not merge:
                tt(wi(48), wi(24), A("c8", 0, 8), ALU.add)
                cp(A(SU, 152, 160), wi(48))
            ts(wi(32), vi, 3, ALU.bitwise_and)
            if not last:
                column(h, vi, wi(40))
            a, b = (0 if merge else 8), (16 if last else 24)
            tt(wi(48 + a, b - a), wi(24 + a, b - a), A("Pw", 40 + a, 40 + b), ALU.add)
            cp(A(SU, 152 + a, 152 + b), wi(48 + a, b - a))
            Xh = IND(A("X", 1024 * h, 1024 * h + 1024), A(SU, 152, 160))
            if CFG["oldS"][h]:
                act(ta, Xh, AF.Copy)
                sm = A("Pu", 256, 384)
                mmg(sm, [(ID, zn), (ID, ta)])
            else:
                sm = A("tf" + H, 256, 384)
                tt(sm, Xh, zn, ALU.add)
            ts(A("ti" + H, 256, 384), sm, 0.5, ALU.mult, -0.25, ALU.add)
            if last:
                ts(wb(24), A(SB, 128, 136), 0.5, ALU.mult, 3.5, ALU.add)
                tt(wb(32), wb(24), A(SB, 144, 152), ALU.subtract)
                for r in range(16):
                    mmg(A("Pw", 64 + r, 192, 16, 0, 8), [(A("Ipad", 16 + r, 144, 16), wb(32))])
                act(A("yso", 128 * h, 128 * h + 128, 1, 0, 8), A("Pw", 64, 192, 1, 0, 8), AF.Copy)
                a, b = 128 * h, 128 * h + 128
                dma("Y", A("yp", a, b), A(SF, 0, 128))
                dma("Y", A("yq", a, b), A(SF, 128, 256))
                dma("Y", A("yz", a, b), zn)
                dma("Y", A("ys", a, b, 1, 0, 8), A("yso", a, b, 1, 0, 8))
            else:
                n1 = lambda n: "%s%d%d" % (n, s + 1, h)
                o1 = add("G", "send1", None, [A(SF, 0, 256)], kind="r", extra=(s, h, A(n1("RF"), 0, 256)))
                o2 = add("G", "send2", None, [A(SU, 0, 176), A(SB, 0, 176)], kind="r", extra=(s, h, A(n1("RU"), 0, 176), A(n1("RB"), 0, 176)))
                o3 = add("N", "recv", A(n1("RF"), 0, 256), [], kind="n", extra=(s, h))
                ops[o3]["wr"] += [(n1("RU"), 0, 176), (n1("RB"), 0, 176)]
                ops[o3]["after"] = [o1, o2]

        def write(h):
            H = str(h)
            tag[0] = "w%d%d" % (s, h)
            cp(IND(A("X", 1024 * h, 1024 * h + 1024), A(nm("SU", h), 152, 160)), A("ti" + H, 256, 384))
            win = A("Dst", 0, 2560) if last and h == 0 else A("Df", 0, 3072)
            cp(IND(win, A(nm("SU", h), 160, 168)), A(nm("RF", h), 256, 384))
            if last:
                dma("Y", A("yx", 1024 * h, 1024 * h + 1024), A("X", 1024 * h, 1024 * h + 1024))
                for q, a in (("Y", 512 * h), ("S" if h else "Y", 1024 + 512 * h)):
                    dma(q, A("yd", a, a + 512), A(win[1], a, a + 512))

        pre(0); pre(1); gathers(0); gathers(1)
        main(0); tail(0); write(0)
        main(1); tail(1); write(1)

    hist, lastbank = {}, {}
    for j, o in enumerate(ops):
        deps = {}
        for (regs, w) in ((o["rd"], False), (o["wr"], True)):
            for (n, a, b) in regs:
                for (i, a2, b2, w2) in hist.get(n, []):
                    if (w or w2) and a < b2 and a2 < b and i != j:
                        deps[i] = not (o["eng"] == "T" and ops[i]["eng"] == "T")
        for (regs, w) in ((o["rd"], False), (o["wr"], True)):
            for (n, a, b) in regs:
                hl = hist.setdefault(n, [])
                if w:
                    hl[:] = [e for e in hl if not (a <= e[1] and e[2] <= b and (o["out"] is None or o["out"][0] == "ind" or o["out"][4] == 1))]
                hl.append((j, a, b, w))
        for bk in o["banks"]:
            if bk in lastbank:
                i = lastbank[bk]
                deps[i] = deps.get(i, False) or ops[i]["eng"] != o["eng"]
            lastbank[bk] = j
        for i in o["after"]:
            deps[i] = False
        o["deps"] = deps
    return ops


def finish(ops, order):
    pos = {j: t for t, j in enumerate(order)}
    need = set()
    for j in order:
        best = {}
        for i, w in ops[j]["deps"].items():
            if w and ops[i]["kind"] == "c" and (ops[i]["eng"] not in best or pos[i] > pos[best[ops[i]["eng"]]]):
                best[ops[i]["eng"]] = i
        ops[j]["wc"] = best
    seen = {e: {} for e in "VSTGYN"}
    for j in order:
        o = ops[j]
        for e2 in list(o["wc"]):
            i = o["wc"][e2]
            if seen[o["eng"]].get(e2, -1) >= pos[i]:
                del o["wc"][e2]
            else:
                seen[o["eng"]][e2] = pos[i]
                need.add(i)
    cnt = {e: 0 for e in "VSTG"}
    nd = 0
    seen = {e: set() for e in "VSTGYN"}
    for j in order:
        o = ops[j]
        o["inc"] = None
        if o["kind"] == "c" and j in need:
            cnt[o["eng"]] += 1
            o["inc"] = ("e" + o["eng"], cnt[o["eng"]])
        elif o["kind"] == "d":
            o["inc"] = ("d%d" % nd, 16)
            nd += 1
        elif o["kind"] == "n":
            o["inc"] = ("r%d%d" % o["extra"], 16)
        ws = [ops[i]["inc"] for i in o["wc"].values()]
        for i, w in o["deps"].items():
            if w and ops[i]["kind"] in "dn" and i not in seen[o["eng"]]:
                seen[o["eng"]].add(i)
                ws.append(ops[i]["inc"])
        o["waits"] = ws
    final = [("e" + e, c) for e, c in cnt.items() if c] + [("d%d" % i, 16) for i in range(nd)]
    final += [("r%d%d" % (s, h), 16) for s in range(STEPS - 1) for h in range(2)] + [("sent", 16 * 2 * (STEPS - 1))]
    return [ops[j] for j in order], final


OPS = build(CFG)
PLAN, FINAL = finish(OPS, schedule(OPS, MID, BIAS, LOOK))
SEMAPHORES = [f[0] for f in FINAL]


def rank_program(g, core, T, topo):
    rank = T.rank_of(core)
    if rank is None:
        return
    queue = {"V": g.vector, "S": g.scalar, "T": g.tensor, "G": g, "Y": g.sync}

    def ap(a):
        if not _isap(a):
            return a
        if a[0] == "ind":
            return ap(a[1]).indirect(ap(a[2]))
        if a[4] == 1:
            return T[a[1]][a[5]:a[6], a[2]:a[3]]
        return T[a[1]][a[5]:a[6], a[2]:a[3]:a[4]]

    def bits(es):
        return sum(1 << e for e in es)

    for o in PLAN:
        if o["kind"] == "n":
            continue
        q = queue[o["eng"]]
        for sem, val in o["waits"]:
            q.wait_ge(T.sem[sem], val)
        m, args = o["meth"], [ap(a) for a in o["args"]]
        kw = {k: ap(v) for k, v in o["kw"].items()}
        if o["kind"] == "r":
            s, h = o["extra"][:2]
            dst = T.cores[(rank + HOP[h]) % len(T.cores)]
            rid, pid, _se = topo.addr(dst)
            es = topo.engines(core, dst)
            rs = T.sem["r%d%d" % (s, h)]
            if m == "send1":
                g.remote_dma(ap(o["extra"][2]), args[0], rs, T.sem.sent, pid, rid, bits(es[0:8]))
            else:
                g.remote_dma_fused([RemoteDMATransfer(dst_ids=[DstId(rid=rid, pnc=pid)], dma_engine_mask=bits(es[8 + 4 * t:12 + 4 * t]),
                                                      remote_sem=rs, src=args[t], dst=ap(o["extra"][2 + t])) for t in range(2)],
                                   local_sem=T.sem.sent)
            continue
        out = ap(o["out"])
        if m == "matmul": ins = q.matmul(out, *args)
        elif m == "activation": ins = q.activation(out, *args, **kw)
        elif m == "tensor_copy": ins = q.tensor_copy(out, *args)
        elif m == "tensor_tensor": ins = q.tensor_tensor(out, *args)
        elif m == "tensor_scalar": ins = q.tensor_scalar(out, *args)
        elif m == "tensor_tensor_scan": ins = q.tensor_tensor_scan(out, *args)
        elif m == "tensor_reduce": ins = q.tensor_reduce(out, *args)
        elif m == "transpose": ins = q.transpose(out, *args)
        elif m == "memset": ins = q.memset(out, *args)
        elif m == "affine_select": ins = q.affine_select(out, *args)
        elif m == "iota": ins = q.iota(out, *args, **kw)
        else: ins = q.dma_start(out, *args)
        if o["inc"] is not None:
            ins.then_inc(T.sem[o["inc"][0]], 16 if o["kind"] == "d" else 1)
    for sem, val in FINAL:
        g.wait_ge(T.sem[sem], val)
